import numpy as np, ml_dtypes
CORES = [71,199,95,223,103,231,111,239,119,247,127,255]
N = 12
NP, TK = 6, 512
def setup_inputs(rng):
    return {"x": rng.standard_normal((N, 128, TK), dtype=np.float32).astype(ml_dtypes.bfloat16), "w1": (rng.standard_normal((N, 128, 128), dtype=np.float32) / 8).astype(ml_dtypes.bfloat16), "w2": (rng.standard_normal((N, 128, NP * 128), dtype=np.float32) / 8).astype(ml_dtypes.bfloat16)}
def setup_inputs_big(rng):
    d = setup_inputs(rng)
    for k in ("x", "w1", "w2"): d[k] = (d[k].astype(np.float32) * 1024.0).astype(d[k].dtype)
    return d
def setup_inputs_small(rng):
    d = setup_inputs(rng)
    for k in ("x", "w1", "w2"): d[k] = (d[k].astype(np.float32) * (1 / 1024.0)).astype(d[k].dtype)
    return d
def setup_inputs_apart(rng):
    d = setup_inputs(rng)
    f = (10.0 ** rng.permutation(np.linspace(-1.5, 1.5, N))).astype(np.float32).reshape(N, 1, 1)
    for k in ("x", "w1", "w2"): d[k] = (d[k].astype(np.float32) * f).astype(d[k].dtype)
    return d
def reference(x, w1, w2):
    X, W1, W2 = x.astype(np.float64), w1.astype(np.float64), w2.astype(np.float64)
    h = [np.maximum(W1[p].T @ X[p], 0.0) for p in range(NP)]
    y = np.full((N, 128, TK), np.nan)
    for q in range(NP, N):
        y[q] = sum(W2[q][:, 128 * p:128 * p + 128].T @ h[p] for p in range(NP))
    return {"y": y.astype(ml_dtypes.bfloat16 if x.dtype != np.float64 else np.float64)}

@@ -1,0 +1,124 @@
+from concourse.bass import DstId, RemoteDMATransfer
+from concourse.mybir import AluOpType
+
+NP, TK, D = 6, 512, 128
+HALF = TK // 2
+
+SCRATCH = {
+    "xs": ("sbuf", [128, TK], "bfloat16"),
+    "w1s": ("sbuf", [128, D], "bfloat16"),
+    "w2s": ("sbuf", [128, NP * D], "bfloat16"),
+    "land": ("sbuf", [128, NP * TK], "bfloat16"),
+    "zero": ("sbuf", [128, HALF], "float32"),
+    "yo": ("sbuf", [128, TK], "bfloat16"),
+    "ps0": ("psum", [128, TK], "float32"),
+    "ps1": ("psum", [128, TK], "float32"),
+}
+SEMAPHORES = ["ldx", "ldw", "zs", "m0", "m1", "c0", "c1", "st0", "st1", "snt"] + ["a%d" % p for p in range(NP)]
+
+
+def _bits(mask):
+    return bin(mask).count("1")
+
+
+def _served(p, far, k):
+    return 2 * ((p // 2 + k) % 3) + (p + far) % 2
+
+
+def _plan(cores, topo):
+    P, Q = cores[:NP], cores[NP:]
+    sends, lands = {}, {}
+    for p, root in enumerate(P):
+        chip = [c for c in range(max(0, root - topo.CORES_PER_CHIP), root + topo.CORES_PER_CHIP)
+                if (topo.host(c), topo.chip(c)) == (topo.host(root), topo.chip(root))]
+        helpers = [c for c in chip if topo.die(c) != topo.die(root) and all(topo.may_write(c, q) for q in Q)]
+        a, b = helpers[0], helpers[1]
+        near = [Q[_served(p, 0, k)] for k in range(3)]
+        far = [Q[_served(p, 1, k)] for k in range(3)]
+        off = topo.mask(root, near[0])
+        for q in near:
+            off &= topo.mask(root, q)
+        stay = topo.mask(root, a) & topo.mask(root, b) & ~off
+        sends[root] = [(p, [(stay, [a])]), (p, [(off, near), (stay, [b])])]
+        sends[a] = [(p, [(topo.mask(a, far[0]) & topo.mask(a, far[1]), far[:2])])]
+        sends[b] = [(p, [(topo.mask(b, far[2]), far[2:])])]
+    for core, calls in sends.items():
+        for p, transfers in calls:
+            for mask, dsts in transfers:
+                for d in dsts:
+                    lands[(d, p)] = _bits(mask)
+    return sends, lands
+
+
+def _issue(g, core, T, topo, calls, lands, wait):
+    total = 0
+    for p, transfers in calls:
+        slot = T.land[:, p * TK:(p + 1) * TK]
+        if wait:
+            g.wait_ge(T.sem["a%d" % p], lands[(core, p)])
+        trs = []
+        for mask, dsts in transfers:
+            ids = []
+            for d in dsts:
+                rid, pid = topo.addr(d, core)
+                ids.append(DstId(rid=rid, pnc=pid))
+            trs.append(RemoteDMATransfer(dst_ids=ids, dma_engine_mask=mask, remote_sem=T.sem["a%d" % p],
+                                         srcs=[slot], dsts=[slot for _ in dsts]))
+            total += _bits(mask)
+        g.remote_dma_fused(trs, local_sem=T.sem.snt)
+    g.wait_ge(T.sem.snt, total)
+
+
+def rank_program(g, core, T, topo):
+    S = T.sem
+    sends, lands = _plan(list(T.cores), topo)
+    rank = T.rank_of(core)
+    ps = [T.ps0, T.ps1]
+    if rank is None:
+        if core in sends:
+            _issue(g, core, T, topo, sends[core], lands, True)
+        return
+
+    if rank < NP:
+        g.sync.dma_start(T.xs[:], T.x[:]).then_inc(S.ldx, 16)
+        g.scalar.dma_start(T.w1s[:], T.w1[:]).then_inc(S.ldw, 16)
+        g.vector.memset(T.zero[:], 0.0).then_inc(S.zs, 1)
+        g.tensor.wait_ge(S.ldw, 16)
+        g.tensor.wait_ge(S.ldx, 16)
+        for h in range(2):
+            g.tensor.matmul(ps[h][:, 0:HALF], T.w1s[:], T.xs[:, h * HALF:(h + 1) * HALF], True, True).then_inc(S["m%d" % h], 1)
+        g.vector.wait_ge(S.zs, 1)
+        for h in range(2):
+            lo = rank * TK + h * HALF
+            g.vector.wait_ge(S["m%d" % h], 1)
+            g.vector.tensor_tensor(T.land[:, lo:lo + HALF], ps[h][:, 0:HALF], T.zero[:], AluOpType.max).then_inc(S["c%d" % h], 1)
+        g.wait_ge(S.c0, 1)
+        g.wait_ge(S.c1, 1)
+        _issue(g, core, T, topo, sends[core], lands, False)
+        return
+
+    j = rank - NP
+    due = {}
+    for p in range(NP):
+        for far in range(2):
+            for k in range(3):
+                if _served(p, far, k) == j:
+                    due[(far, k)] = p
+    order = [due[t] for t in ((0, 0), (0, 1), (1, 0), (0, 2), (1, 1), (1, 2))]
+    g.sync.dma_start(T.w2s[:], T.w2[:]).then_inc(S.ldw, 16)
+    g.tensor.wait_ge(S.ldw, 16)
+    for i, p in enumerate(order):
+        g.tensor.wait_ge(S["a%d" % p], lands[(core, p)])
+        for h in range(2):
+            lo = p * TK + h * HALF
+            mm = g.tensor.matmul(ps[h][:, 0:HALF], T.w2s[:, p * D:(p + 1) * D], T.land[:, lo:lo + HALF], i == 0, i == NP - 1)
+            if i == NP - 1:
+                mm.then_inc(S["m%d" % h], 1)
+    queues = [g.sync, g.scalar]
+    for h in range(2):
+        g.vector.wait_ge(S["m%d" % h], 1)
+        g.vector.tensor_copy(T.yo[:, h * HALF:(h + 1) * HALF], ps[h][:, 0:HALF]).then_inc(S["c%d" % h], 1)
+    for h in range(2):
+        queues[h].wait_ge(S["c%d" % h], 1)
+        queues[h].dma_start(T.y[:, h * HALF:(h + 1) * HALF], T.yo[:, h * HALF:(h + 1) * HALF]).then_inc(S["st%d" % h], 16)
+        queues[h].wait_ge(S["st%d" % h], 16)

@@ -2,19 +2,24 @@ from concourse.bass import DstId, RemoteDMATransfer
 from concourse.mybir import AluOpType
 
 NP, TK, D = 6, 512, 128
-HALF = TK // 2
+DIRECT = 2
+CUTS = [0, 64, 288, 512]
+LEAD = CUTS[1]
+WIDEST = max(CUTS[i + 1] - CUTS[i] for i in range(3))
 
 SCRATCH = {
     "xs": ("sbuf", [128, TK], "bfloat16"),
     "w1s": ("sbuf", [128, D], "bfloat16"),
     "w2s": ("sbuf", [128, NP * D], "bfloat16"),
     "land": ("sbuf", [128, NP * TK], "bfloat16"),
-    "zero": ("sbuf", [128, HALF], "float32"),
+    "zero": ("sbuf", [128, WIDEST], "float32"),
     "yo": ("sbuf", [128, TK], "bfloat16"),
     "ps0": ("psum", [128, TK], "float32"),
     "ps1": ("psum", [128, TK], "float32"),
+    "ps2": ("psum", [128, TK], "float32"),
 }
-SEMAPHORES = ["ldx", "ldw", "zs", "m0", "m1", "c0", "c1", "st0", "st1", "snt"] + ["a%d" % p for p in range(NP)]
+SEMAPHORES = (["ldx0", "ldx", "ldw", "zs", "m0", "m1", "m2", "c0", "c1", "c2", "st0", "st1", "st2", "snt", "f0", "f1"]
+              + ["a%d" % p for p in range(NP)] + ["b%d" % p for p in range(NP)])
 
 
 def _bits(mask):
@@ -31,41 +36,45 @@ def _plan(cores, topo):
     for p, root in enumerate(P):
         chip = [c for c in range(max(0, root - topo.CORES_PER_CHIP), root + topo.CORES_PER_CHIP)
                 if (topo.host(c), topo.chip(c)) == (topo.host(root), topo.chip(root))]
-        helpers = [c for c in chip if topo.die(c) != topo.die(root) and all(topo.may_write(c, q) for q in Q)]
-        a, b = helpers[0], helpers[1]
         near = [Q[_served(p, 0, k)] for k in range(3)]
         far = [Q[_served(p, 1, k)] for k in range(3)]
-        off = topo.mask(root, near[0])
-        for q in near:
+        helpers = []
+        for d in far + near[DIRECT:]:
+            cand = [c for c in chip if c != root and c not in helpers and topo.may_write(c, d)
+                    and (topo.die(c) != topo.die(root)) == (d in far)]
+            cand.sort(key=lambda c: sum(1 for q in Q if topo.may_write(c, q)))
+            helpers.append(cand[0])
+            m = topo.mask(cand[0], d)
+            sends[cand[0]] = [(["f0"], p, 0, LEAD, "a%d" % p, m, [d]), (["f1"], p, LEAD, TK, "b%d" % p, m, [d])]
+        off, stay = topo.mask(root, near[0]), topo.mask(root, helpers[0])
+        for q in near[:DIRECT]:
             off &= topo.mask(root, q)
-        stay = topo.mask(root, a) & topo.mask(root, b) & ~off
-        sends[root] = [(p, [(stay, [a])]), (p, [(off, near), (stay, [b])])]
-        sends[a] = [(p, [(topo.mask(a, far[0]) & topo.mask(a, far[1]), far[:2])])]
-        sends[b] = [(p, [(topo.mask(b, far[2]), far[2:])])]
+        for c in helpers:
+            stay &= topo.mask(root, c)
+        stay &= ~off
+        sends[root] = [(["c0"], p, 0, LEAD, "f0", stay, helpers),
+                       (["c1", "c2"], p, 0, TK, "a%d" % p, off, near[:DIRECT]),
+                       ([], p, LEAD, TK, "f1", stay, helpers)]
     for core, calls in sends.items():
-        for p, transfers in calls:
-            for mask, dsts in transfers:
-                for d in dsts:
-                    lands[(d, p)] = _bits(mask)
+        for waits, p, lo, hi, sem, mask, dsts in calls:
+            for d in dsts:
+                lands[(d, sem)] = lands.get((d, sem), 0) + _bits(mask)
     return sends, lands
 
 
-def _issue(g, core, T, topo, calls, lands, wait):
+def _issue(g, core, T, topo, calls, lands):
     total = 0
-    for p, transfers in calls:
-        slot = T.land[:, p * TK:(p + 1) * TK]
-        if wait:
-            g.wait_ge(T.sem["a%d" % p], lands[(core, p)])
-        trs = []
-        for mask, dsts in transfers:
-            ids = []
-            for d in dsts:
-                rid, pid = topo.addr(d, core)
-                ids.append(DstId(rid=rid, pnc=pid))
-            trs.append(RemoteDMATransfer(dst_ids=ids, dma_engine_mask=mask, remote_sem=T.sem["a%d" % p],
-                                         srcs=[slot], dsts=[slot for _ in dsts]))
-            total += _bits(mask)
-        g.remote_dma_fused(trs, local_sem=T.sem.snt)
+    for waits, p, lo, hi, sem, mask, dsts in calls:
+        piece = T.land[:, p * TK + lo:p * TK + hi]
+        for w in waits:
+            g.wait_ge(T.sem[w], lands.get((core, w), 1))
+        ids = []
+        for d in dsts:
+            rid, pid = topo.addr(d, core)
+            ids.append(DstId(rid=rid, pnc=pid))
+        g.remote_dma_fused([RemoteDMATransfer(dst_ids=ids, dma_engine_mask=mask, remote_sem=T.sem[sem],
+                                              srcs=[piece], dsts=[piece for _ in dsts])], local_sem=T.sem.snt)
+        total += _bits(mask)
     g.wait_ge(T.sem.snt, total)
 
 
@@ -73,28 +82,31 @@ def rank_program(g, core, T, topo):
     S = T.sem
     sends, lands = _plan(list(T.cores), topo)
     rank = T.rank_of(core)
-    ps = [T.ps0, T.ps1]
+    ps = [T.ps0, T.ps1, T.ps2]
     if rank is None:
         if core in sends:
-            _issue(g, core, T, topo, sends[core], lands, True)
+            _issue(g, core, T, topo, sends[core], lands)
         return
 
     if rank < NP:
-        g.sync.dma_start(T.xs[:], T.x[:]).then_inc(S.ldx, 16)
+        g.sync.dma_start(T.xs[:, 0:LEAD], T.x[:, 0:LEAD]).then_inc(S.ldx0, 16)
         g.scalar.dma_start(T.w1s[:], T.w1[:]).then_inc(S.ldw, 16)
+        g.sync.dma_start(T.xs[:, LEAD:TK], T.x[:, LEAD:TK]).then_inc(S.ldx, 16)
         g.vector.memset(T.zero[:], 0.0).then_inc(S.zs, 1)
         g.tensor.wait_ge(S.ldw, 16)
-        g.tensor.wait_ge(S.ldx, 16)
-        for h in range(2):
-            g.tensor.matmul(ps[h][:, 0:HALF], T.w1s[:], T.xs[:, h * HALF:(h + 1) * HALF], True, True).then_inc(S["m%d" % h], 1)
+        g.tensor.wait_ge(S.ldx0, 16)
+        for i in range(3):
+            lo, hi = CUTS[i], CUTS[i + 1]
+            if i == 1:
+                g.tensor.wait_ge(S.ldx, 16)
+            g.tensor.matmul(ps[i][:, 0:hi - lo], T.w1s[:], T.xs[:, lo:hi], True, True).then_inc(S["m%d" % i], 1)
         g.vector.wait_ge(S.zs, 1)
-        for h in range(2):
-            lo = rank * TK + h * HALF
-            g.vector.wait_ge(S["m%d" % h], 1)
-            g.vector.tensor_tensor(T.land[:, lo:lo + HALF], ps[h][:, 0:HALF], T.zero[:], AluOpType.max).then_inc(S["c%d" % h], 1)
-        g.wait_ge(S.c0, 1)
-        g.wait_ge(S.c1, 1)
-        _issue(g, core, T, topo, sends[core], lands, False)
+        for i in range(3):
+            lo, hi = CUTS[i], CUTS[i + 1]
+            g.vector.wait_ge(S["m%d" % i], 1)
+            g.vector.tensor_tensor(T.land[:, rank * TK + lo:rank * TK + hi], ps[i][:, 0:hi - lo], T.zero[:, 0:hi - lo],
+                                   AluOpType.max).then_inc(S["c%d" % i], 1)
+        _issue(g, core, T, topo, sends[core], lands)
         return
 
     j = rank - NP
@@ -104,21 +116,32 @@ def rank_program(g, core, T, topo):
             for k in range(3):
                 if _served(p, far, k) == j:
                     due[(far, k)] = p
-    order = [due[t] for t in ((0, 0), (0, 1), (1, 0), (0, 2), (1, 1), (1, 2))]
+    whole = [due[(0, k)] for k in range(DIRECT)]
+    split = [due[(1, k)] for k in range(3)] + [due[(0, k)] for k in range(DIRECT, 3)]
+    work = ([("a%d" % p, p, (0, 1, 2)) for p in whole] + [("a%d" % p, p, (0,)) for p in split]
+            + [("b%d" % p, p, (1, 2)) for p in split])
+    last = {}
+    for n, (sem, p, pieces) in enumerate(work):
+        for i in pieces:
+            last[i] = n
     g.sync.dma_start(T.w2s[:], T.w2[:]).then_inc(S.ldw, 16)
     g.tensor.wait_ge(S.ldw, 16)
-    for i, p in enumerate(order):
-        g.tensor.wait_ge(S["a%d" % p], lands[(core, p)])
-        for h in range(2):
-            lo = p * TK + h * HALF
-            mm = g.tensor.matmul(ps[h][:, 0:HALF], T.w2s[:, p * D:(p + 1) * D], T.land[:, lo:lo + HALF], i == 0, i == NP - 1)
-            if i == NP - 1:
-                mm.then_inc(S["m%d" % h], 1)
-    queues = [g.sync, g.scalar]
-    for h in range(2):
-        g.vector.wait_ge(S["m%d" % h], 1)
-        g.vector.tensor_copy(T.yo[:, h * HALF:(h + 1) * HALF], ps[h][:, 0:HALF]).then_inc(S["c%d" % h], 1)
-    for h in range(2):
-        queues[h].wait_ge(S["c%d" % h], 1)
-        queues[h].dma_start(T.y[:, h * HALF:(h + 1) * HALF], T.yo[:, h * HALF:(h + 1) * HALF]).then_inc(S["st%d" % h], 16)
-        queues[h].wait_ge(S["st%d" % h], 16)
+    for n, (sem, p, pieces) in enumerate(work):
+        g.tensor.wait_ge(S[sem], lands[(core, sem)])
+        for i in pieces:
+            lo, hi = CUTS[i], CUTS[i + 1]
+            mm = g.tensor.matmul(ps[i][:, 0:hi - lo], T.w2s[:, p * D:(p + 1) * D], T.land[:, p * TK + lo:p * TK + hi],
+                                 n == 0, n == last[i])
+            if n == last[i]:
+                mm.then_inc(S["m%d" % i], 1)
+    for i in range(3):
+        lo, hi = CUTS[i], CUTS[i + 1]
+        g.vector.wait_ge(S["m%d" % i], 1)
+        g.vector.tensor_copy(T.yo[:, lo:hi], ps[i][:, 0:hi - lo]).then_inc(S["c%d" % i], 1)
+    queues = [g.sync, g.scalar, g.sync]
+    for i in range(3):
+        lo, hi = CUTS[i], CUTS[i + 1]
+        queues[i].wait_ge(S["c%d" % i], 1)
+        queues[i].dma_start(T.y[:, lo:hi], T.yo[:, lo:hi]).then_inc(S["st%d" % i], 16)
+    for i in range(3):
+        queues[i].wait_ge(S["st%d" % i], 16)

@@ -4,7 +4,7 @@ from concourse.mybir import AluOpType
 NP, TK, D = 6, 512, 128
 DIRECT = 2
 CUTS = [0, 64, 288, 512]
-LEAD = CUTS[1]
+LEAD, MID = CUTS[1], CUTS[2]
 WIDEST = max(CUTS[i + 1] - CUTS[i] for i in range(3))
 
 SCRATCH = {
@@ -18,8 +18,8 @@ SCRATCH = {
     "ps1": ("psum", [128, TK], "float32"),
     "ps2": ("psum", [128, TK], "float32"),
 }
-SEMAPHORES = (["ldx0", "ldx", "ldw", "zs", "m0", "m1", "m2", "c0", "c1", "c2", "st0", "st1", "st2", "snt", "f0", "f1"]
-              + ["a%d" % p for p in range(NP)] + ["b%d" % p for p in range(NP)])
+SEMAPHORES = (["ldx0", "ldx", "ldw", "zs", "m0", "m1", "m2", "c0", "c1", "c2", "st0", "st1", "st2", "snt", "f0", "f1", "f2"]
+              + ["a%d" % p for p in range(NP)] + ["k%d" % p for p in range(NP)] + ["b%d" % p for p in range(NP)])
 
 
 def _bits(mask):
@@ -45,36 +45,45 @@ def _plan(cores, topo):
             cand.sort(key=lambda c: sum(1 for q in Q if topo.may_write(c, q)))
             helpers.append(cand[0])
             m = topo.mask(cand[0], d)
-            sends[cand[0]] = [(["f0"], p, 0, LEAD, "a%d" % p, m, [d]), (["f1"], p, LEAD, TK, "b%d" % p, m, [d])]
-        off, stay = topo.mask(root, near[0]), topo.mask(root, helpers[0])
-        for q in near[:DIRECT]:
+            sends[cand[0]] = [(["f0"], [(p, 0, LEAD, "a%d" % p, m, [d])]), (["f1"], [(p, LEAD, MID, "k%d" % p, m, [d])])]
+            if d != far[2]:
+                sends[cand[0]].append((["f2"], [(p, MID, TK, "b%d" % p, m, [d])]))
+        own = near[:DIRECT] + [far[2]]
+        off, stay = topo.mask(root, own[0]), topo.mask(root, helpers[0])
+        for q in own:
             off &= topo.mask(root, q)
         for c in helpers:
             stay &= topo.mask(root, c)
         stay &= ~off
-        sends[root] = [(["c0"], p, 0, LEAD, "f0", stay, helpers),
-                       (["c1", "c2"], p, 0, TK, "a%d" % p, off, near[:DIRECT]),
-                       ([], p, LEAD, TK, "f1", stay, helpers)]
+        sends[root] = [(["c0"], [(p, 0, LEAD, "f0", stay, helpers)]),
+                       (["c1"], [(p, LEAD, MID, "f1", stay, helpers)]),
+                       (["c2"], [(p, MID, TK, "f2", stay, helpers[0:2] + helpers[3:]),
+                                 (p, MID, TK, "b%d" % p, off, [far[2]])]),
+                       ([], [(p, 0, TK, "a%d" % p, off, near[:DIRECT])])]
     for core, calls in sends.items():
-        for waits, p, lo, hi, sem, mask, dsts in calls:
-            for d in dsts:
-                lands[(d, sem)] = lands.get((d, sem), 0) + _bits(mask)
+        for waits, transfers in calls:
+            for p, lo, hi, sem, mask, dsts in transfers:
+                for d in dsts:
+                    lands[(d, sem)] = lands.get((d, sem), 0) + _bits(mask)
     return sends, lands
 
 
 def _issue(g, core, T, topo, calls, lands):
     total = 0
-    for waits, p, lo, hi, sem, mask, dsts in calls:
-        piece = T.land[:, p * TK + lo:p * TK + hi]
+    for waits, transfers in calls:
         for w in waits:
             g.wait_ge(T.sem[w], lands.get((core, w), 1))
-        ids = []
-        for d in dsts:
-            rid, pid = topo.addr(d, core)
-            ids.append(DstId(rid=rid, pnc=pid))
-        g.remote_dma_fused([RemoteDMATransfer(dst_ids=ids, dma_engine_mask=mask, remote_sem=T.sem[sem],
-                                              srcs=[piece], dsts=[piece for _ in dsts])], local_sem=T.sem.snt)
-        total += _bits(mask)
+        made = []
+        for p, lo, hi, sem, mask, dsts in transfers:
+            piece = T.land[:, p * TK + lo:p * TK + hi]
+            ids = []
+            for d in dsts:
+                rid, pid = topo.addr(d, core)
+                ids.append(DstId(rid=rid, pnc=pid))
+            made.append(RemoteDMATransfer(dst_ids=ids, dma_engine_mask=mask, remote_sem=T.sem[sem],
+                                          srcs=[piece], dsts=[piece for _ in dsts]))
+            total += _bits(mask)
+        g.remote_dma_fused(made, local_sem=T.sem.snt)
     g.wait_ge(T.sem.snt, total)
 
 
@@ -118,11 +127,14 @@ def rank_program(g, core, T, topo):
                     due[(far, k)] = p
     whole = [due[(0, k)] for k in range(DIRECT)]
     split = [due[(1, k)] for k in range(3)] + [due[(0, k)] for k in range(DIRECT, 3)]
-    work = ([("a%d" % p, p, (0, 1, 2)) for p in whole] + [("a%d" % p, p, (0,)) for p in split]
-            + [("b%d" % p, p, (1, 2)) for p in split])
-    last = {}
+    late = [p for p in split if p != due[(1, 2)]]
+    work = ([("b%d" % due[(1, 2)], due[(1, 2)], (2,))] + [("a%d" % p, p, (0, 1, 2)) for p in whole]
+            + [("a%d" % p, p, (0,)) for p in split] + [("k%d" % p, p, (1,)) for p in split]
+            + [("b%d" % p, p, (2,)) for p in late])
+    first, last = {}, {}
     for n, (sem, p, pieces) in enumerate(work):
         for i in pieces:
+            first.setdefault(i, n)
             last[i] = n
     g.sync.dma_start(T.w2s[:], T.w2[:]).then_inc(S.ldw, 16)
     g.tensor.wait_ge(S.ldw, 16)
@@ -131,7 +143,7 @@ def rank_program(g, core, T, topo):
         for i in pieces:
             lo, hi = CUTS[i], CUTS[i + 1]
             mm = g.tensor.matmul(ps[i][:, 0:hi - lo], T.w2s[:, p * D:(p + 1) * D], T.land[:, p * TK + lo:p * TK + hi],
-                                 n == 0, n == last[i])
+                                 n == first[i], n == last[i])
             if n == last[i]:
                 mm.then_inc(S["m%d" % i], 1)
     for i in range(3):

from concourse.bass import DstId, RemoteDMATransfer
from concourse.mybir import AluOpType

NP, TK, D = 6, 512, 128
DIRECT = 2
CUTS = [0, 64, 288, 512]
LEAD, MID = CUTS[1], CUTS[2]
WIDEST = max(CUTS[i + 1] - CUTS[i] for i in range(3))

SCRATCH = {
    "xs": ("sbuf", [128, TK], "bfloat16"),
    "w1s": ("sbuf", [128, D], "bfloat16"),
    "w2s": ("sbuf", [128, NP * D], "bfloat16"),
    "land": ("sbuf", [128, NP * TK], "bfloat16"),
    "zero": ("sbuf", [128, WIDEST], "float32"),
    "yo": ("sbuf", [128, TK], "bfloat16"),
    "ps0": ("psum", [128, TK], "float32"),
    "ps1": ("psum", [128, TK], "float32"),
    "ps2": ("psum", [128, TK], "float32"),
}
SEMAPHORES = (["ldx0", "ldx", "ldw", "zs", "m0", "m1", "m2", "c0", "c1", "c2", "st0", "st1", "st2", "snt", "f0", "f1", "f2"]
              + ["a%d" % p for p in range(NP)] + ["k%d" % p for p in range(NP)] + ["b%d" % p for p in range(NP)])


def _bits(mask):
    return bin(mask).count("1")


def _served(p, far, k):
    return 2 * ((p // 2 + k) % 3) + (p + far) % 2


def _plan(cores, topo):
    P, Q = cores[:NP], cores[NP:]
    sends, lands = {}, {}
    for p, root in enumerate(P):
        chip = [c for c in range(max(0, root - topo.CORES_PER_CHIP), root + topo.CORES_PER_CHIP)
                if (topo.host(c), topo.chip(c)) == (topo.host(root), topo.chip(root))]
        near = [Q[_served(p, 0, k)] for k in range(3)]
        far = [Q[_served(p, 1, k)] for k in range(3)]
        helpers = []
        for d in far + near[DIRECT:]:
            cand = [c for c in chip if c != root and c not in helpers and topo.may_write(c, d)
                    and (topo.die(c) != topo.die(root)) == (d in far)]
            cand.sort(key=lambda c: sum(1 for q in Q if topo.may_write(c, q)))
            helpers.append(cand[0])
            m = topo.mask(cand[0], d)
            sends[cand[0]] = [(["f0"], [(p, 0, LEAD, "a%d" % p, m, [d])]), (["f1"], [(p, LEAD, MID, "k%d" % p, m, [d])])]
            if d != far[2]:
                sends[cand[0]].append((["f2"], [(p, MID, TK, "b%d" % p, m, [d])]))
        own = near[:DIRECT] + [far[2]]
        off, stay = topo.mask(root, own[0]), topo.mask(root, helpers[0])
        for q in own:
            off &= topo.mask(root, q)
        for c in helpers:
            stay &= topo.mask(root, c)
        stay &= ~off
        sends[root] = [(["c0"], [(p, 0, LEAD, "f0", stay, helpers)]),
                       (["c1"], [(p, LEAD, MID, "f1", stay, helpers)]),
                       (["c2"], [(p, MID, TK, "f2", stay, helpers[0:2] + helpers[3:]),
                                 (p, MID, TK, "b%d" % p, off, [far[2]])]),
                       ([], [(p, 0, TK, "a%d" % p, off, near[:DIRECT])])]
    for core, calls in sends.items():
        for waits, transfers in calls:
            for p, lo, hi, sem, mask, dsts in transfers:
                for d in dsts:
                    lands[(d, sem)] = lands.get((d, sem), 0) + _bits(mask)
    return sends, lands


def _issue(g, core, T, topo, calls, lands):
    total = 0
    for waits, transfers in calls:
        for w in waits:
            g.wait_ge(T.sem[w], lands.get((core, w), 1))
        made = []
        for p, lo, hi, sem, mask, dsts in transfers:
            piece = T.land[:, p * TK + lo:p * TK + hi]
            ids = []
            for d in dsts:
                rid, pid = topo.addr(d, core)
                ids.append(DstId(rid=rid, pnc=pid))
            made.append(RemoteDMATransfer(dst_ids=ids, dma_engine_mask=mask, remote_sem=T.sem[sem],
                                          srcs=[piece], dsts=[piece for _ in dsts]))
            total += _bits(mask)
        g.remote_dma_fused(made, local_sem=T.sem.snt)
    g.wait_ge(T.sem.snt, total)


def rank_program(g, core, T, topo):
    S = T.sem
    sends, lands = _plan(list(T.cores), topo)
    rank = T.rank_of(core)
    ps = [T.ps0, T.ps1, T.ps2]
    if rank is None:
        if core in sends:
            _issue(g, core, T, topo, sends[core], lands)
        return

    if rank < NP:
        g.sync.dma_start(T.xs[:, 0:LEAD], T.x[:, 0:LEAD]).then_inc(S.ldx0, 16)
        g.scalar.dma_start(T.w1s[:], T.w1[:]).then_inc(S.ldw, 16)
        g.sync.dma_start(T.xs[:, LEAD:TK], T.x[:, LEAD:TK]).then_inc(S.ldx, 16)
        g.vector.memset(T.zero[:], 0.0).then_inc(S.zs, 1)
        g.tensor.wait_ge(S.ldw, 16)
        g.tensor.wait_ge(S.ldx0, 16)
        for i in range(3):
            lo, hi = CUTS[i], CUTS[i + 1]
            if i == 1:
                g.tensor.wait_ge(S.ldx, 16)
            g.tensor.matmul(ps[i][:, 0:hi - lo], T.w1s[:], T.xs[:, lo:hi], True, True).then_inc(S["m%d" % i], 1)
        g.vector.wait_ge(S.zs, 1)
        for i in range(3):
            lo, hi = CUTS[i], CUTS[i + 1]
            g.vector.wait_ge(S["m%d" % i], 1)
            g.vector.tensor_tensor(T.land[:, rank * TK + lo:rank * TK + hi], ps[i][:, 0:hi - lo], T.zero[:, 0:hi - lo],
                                   AluOpType.max).then_inc(S["c%d" % i], 1)
        _issue(g, core, T, topo, sends[core], lands)
        return

    j = rank - NP
    due = {}
    for p in range(NP):
        for far in range(2):
            for k in range(3):
                if _served(p, far, k) == j:
                    due[(far, k)] = p
    whole = [due[(0, k)] for k in range(DIRECT)]
    split = [due[(1, k)] for k in range(3)] + [due[(0, k)] for k in range(DIRECT, 3)]
    late = [p for p in split if p != due[(1, 2)]]
    work = ([("b%d" % due[(1, 2)], due[(1, 2)], (2,))] + [("a%d" % p, p, (0, 1, 2)) for p in whole]
            + [("a%d" % p, p, (0,)) for p in split] + [("k%d" % p, p, (1,)) for p in split]
            + [("b%d" % p, p, (2,)) for p in late])
    first, last = {}, {}
    for n, (sem, p, pieces) in enumerate(work):
        for i in pieces:
            first.setdefault(i, n)
            last[i] = n
    g.sync.dma_start(T.w2s[:], T.w2[:]).then_inc(S.ldw, 16)
    g.tensor.wait_ge(S.ldw, 16)
    for n, (sem, p, pieces) in enumerate(work):
        g.tensor.wait_ge(S[sem], lands[(core, sem)])
        for i in pieces:
            lo, hi = CUTS[i], CUTS[i + 1]
            mm = g.tensor.matmul(ps[i][:, 0:hi - lo], T.w2s[:, p * D:(p + 1) * D], T.land[:, p * TK + lo:p * TK + hi],
                                 n == first[i], n == last[i])
            if n == last[i]:
                mm.then_inc(S["m%d" % i], 1)
    for i in range(3):
        lo, hi = CUTS[i], CUTS[i + 1]
        g.vector.wait_ge(S["m%d" % i], 1)
        g.vector.tensor_copy(T.yo[:, lo:hi], ps[i][:, 0:hi - lo]).then_inc(S["c%d" % i], 1)
    queues = [g.sync, g.scalar, g.sync]
    for i in range(3):
        lo, hi = CUTS[i], CUTS[i + 1]
        queues[i].wait_ge(S["c%d" % i], 1)
        queues[i].dma_start(T.y[:, lo:hi], T.yo[:, lo:hi]).then_inc(S["st%d" % i], 16)
    for i in range(3):
        queues[i].wait_ge(S["st%d" % i], 16)
